import numpy as np
import ml_dtypes


def mxq(x, axis, fmt="e4m3"):
    dtype, down = {"e4m3": (ml_dtypes.float8_e4m3fn, 7), "e5m2": (ml_dtypes.float8_e5m2, 14)}[fmt]
    v = np.moveaxis(np.asarray(x, np.float32).astype(ml_dtypes.bfloat16).astype(np.float64), axis, -1)
    blocks = v.reshape(v.shape[:-1] + (-1, 32))
    amax = np.abs(blocks).max(-1, keepdims=True)
    byte = np.maximum(np.where(amax > 0, np.frexp(amax)[1] - 1 + 127, 0) - down, 1)
    scale = np.exp2(byte - 127.0)
    codes = (blocks / scale).astype(np.float32).astype(dtype).astype(np.float64)
    return np.moveaxis((codes * scale).reshape(v.shape), -1, axis)


WIDE = False


def mx_kscale(k):
    if not WIDE:
        return np.ones(k)
    levels = np.array([10, -10, 5, -5, 0])
    if k % 512:
        return np.exp2(np.random.permutation(np.resize(levels, k // 32))).repeat(32)
    a = np.empty((k // 512, 16))
    for p in range(k // 512):
        a[p, :8] = np.random.permutation(np.resize(levels, 8))
        for g in range(8):
            far = levels[np.abs(levels - a[p, g]) >= 10]
            a[p, g + 8] = far[np.random.randint(len(far))]
    return np.exp2(a.ravel()).repeat(32)


def f64(x):
    return np.asarray(x).astype(np.float64)


def striped8(idx):
    return np.concatenate([v.reshape(-1, 16).T for v in idx]).astype(np.uint16)


def unstriped8(offs):
    return np.stack([offs[16 * g:16 * g + 16].T.reshape(-1) for g in range(8)]).astype(np.int64)


E2M1 = np.array([0.0, 0.5, 1.0, 1.5, 2.0, 3.0, 4.0, 6.0, -0.0, -0.5, -1.0, -1.5, -2.0, -3.0, -4.0, -6.0])


def pack_weight(w, fmt):
    k, n = w.shape
    w = f64(np.asarray(w, np.float32).astype(ml_dtypes.bfloat16)).reshape(k // 32, 32, n)
    amax = np.abs(w).max(1)
    if fmt == "e4m3":
        byte = np.frexp(amax)[1] - 1 + 127 - 7
    else:
        mant, ex = np.frexp(amax / 6.0)
        byte = np.where(mant > 0.5, ex, ex - 1) + 127
    byte = np.clip(np.where(amax > 0, byte, 1), 1, 254)
    scaled = (w * np.exp2(127.0 - byte)[:, None, :]).reshape(k, n).astype(np.float32)
    by_word = np.ascontiguousarray(scaled.reshape(k // 512, 128, 4, n).transpose(0, 1, 3, 2))
    if fmt == "e4m3":
        words = by_word.astype(ml_dtypes.float8_e4m3fn).view(np.uint8)
    else:
        c = by_word.astype(ml_dtypes.float4_e2m1fn).view(np.uint8) & 0xF
        words = (c[..., 0::2] | (c[..., 1::2] << 4)).reshape(k // 512, 128, 2 * n)
    return np.ascontiguousarray(words), np.ascontiguousarray(byte.astype(np.uint8).reshape(k // 512, 16, n))


def unpack_weight(words, scales, fmt):
    g, _, n = scales.shape
    words = np.ascontiguousarray(words).reshape(g, 128, n, -1)
    if fmt == "e4m3":
        vals = words.view(ml_dtypes.float8_e4m3fn).astype(np.float64)
    else:
        nib = np.empty((g, 128, n, 4), np.uint8)
        nib[..., 0::2] = words & 0xF
        nib[..., 1::2] = words >> 4
        vals = E2M1[nib]
    vals = vals * np.repeat(np.exp2(scales.astype(np.float64) - 127.0), 8, axis=1)[..., None]
    return vals.transpose(0, 1, 3, 2).reshape(g * 512, n)


def silu(v):
    return v / (1.0 + np.exp(-np.maximum(v, -700.0)))


K, M, T, S = 1024, 1024, 4096, 2048


def setup_inputs():
    n = np.random.standard_normal
    s = mx_kscale(K)[:, None]
    u = mx_kscale(512)[:, None]
    p_w4 = pack_weight(n((K, M)) / np.sqrt(K) / s, "e2m1")
    return {
        "x": (n((K, S)) * s).astype(np.float32),
        "w4_words": p_w4[0],
        "w4_scales": p_w4[1],
        "down": (n((K, 512)) / np.sqrt(K) / s * u.T).astype(np.float32),
        "up": (0.5 * n((512, M)) / np.sqrt(512) / u).astype(np.float32),
        "b": (0.3 * n(1024)).astype(np.float32),
        "wgo": np.repeat(np.random.uniform(0.5, 2.0, (8, S)), 16, axis=0).astype(np.float32),
        "offs": striped8(np.stack([np.random.permutation(T)[:S] for _ in range(8)])),
    }


def reference(x, w4_words, w4_scales, down, up, b, wgo, offs):
    x_ = mxq(f64(x), 0, "e4m3")
    w4_ = unpack_weight(w4_words, w4_scales, "e2m1")
    down_ = mxq(f64(down), 0, "e4m3")
    up_ = mxq(f64(up), 0, "e4m3")
    h_ = mxq(down_.T @ x_, 0, "e4m3")
    y = w4_.T @ x_ + up_.T @ h_
    place = unstriped8(offs)[np.arange(M) % 128 // 16]
    out = np.zeros((M, T))
    out[np.arange(M)[:, None], place] = f64(wgo)[np.arange(M) % 128] * (silu(y + f64(b)[:, None]))
    return out

@@ -1,0 +1,295 @@
+from contextlib import ExitStack
+
+import concourse.mybir as mybir
+from concourse.masks import make_identity
+
+K, M, T, S, R = 1024, 1024, 4096, 2048, 512
+FLOPS = 2 * S * (K * R + K * M + R * M)
+
+F32 = mybir.dt.float32
+BF16 = mybir.dt.bfloat16
+I32 = mybir.dt.int32
+U32 = mybir.dt.uint32
+U16 = mybir.dt.uint16
+U8 = mybir.dt.uint8
+FP8X4 = mybir.dt.float8_e4m3fn_x4
+FP4X4 = mybir.dt.float4_e2m1fn_x4
+SILU = mybir.ActivationFunctionType.Silu
+MULT = mybir.AluOpType.mult
+
+P = 128
+PACK = 4
+K_PASS = P * PACK
+PASSES = K // K_PASS
+BANK = 512
+LIST_ROWS = 16
+W = 256
+ROUNDS = S // W
+EARLY = 3
+UP_PARTS = [(0, 256), (256, 384), (384, 640), (640, 896), (896, 1024)]
+
+
+def tile_list_hscat_l_silu_kernel(tc, x, w4_words, w4_scales, down, up, b, wgo, offs, out):
+    nc = tc.nc
+    with ExitStack() as ctx:
+        keep = ctx.enter_context(tc.tile_pool(name="keep", bufs=1))
+        psum = ctx.enter_context(tc.psum_pool(name="psum", bufs=1))
+
+        def sb(name, shape, dtype):
+            return keep.tile(shape, dtype, name=name, align_bytes=64)
+
+        def slots(ap):
+            return ap.rearrange("p (t c) -> p t c", t=PACK)
+
+        lists = keep.tile([P, S // LIST_ROWS], U16, name="lists")
+        pages = [sb("page%d" % i, [P, T], F32) for i in range(EARLY)]
+        acts = [sb("act%d" % i, [P, S], F32) for i in range(2)]
+        weights = sb("weights", [P, S], F32)
+        shared = keep.tile([P, T], F32, name="shared", tag="shared", align_bytes=64)
+        down_raw = [shared[:, a * PACK * R : (a + 1) * PACK * R] for a in range(PASSES)]
+        x_raw = {}
+        for r in range(ROUNDS):
+            for a in range(PASSES):
+                if r < ROUNDS - 2:
+                    x_raw[r, a] = sb("x_raw%d_%d" % (r, a), [P, PACK * W], F32)[:]
+                else:
+                    first = (PASSES * (r - ROUNDS + 2) + a) * PACK * W
+                    x_raw[r, a] = shared[:, first : first + PACK * W]
+        up_raw = [sb("up_raw%d" % i, [P, PACK * (n1 - n0)], F32)[:] for i, (n0, n1) in enumerate(UP_PARTS)]
+        stage = [sb("stage%d" % i, [P, PASSES * PACK * W], BF16) for i in range(2)]
+        down_stage = [sb("down_stage%d" % a, [P, PACK * R], BF16) for a in range(PASSES)]
+        up_stage = sb("up_stage", [P, PACK * EARLY * P], BF16)
+        h_stage = [sb("h_stage%d" % i, [P, PACK * W], BF16) for i in range(2)]
+        x_codes = sb("x_codes", [P, PASSES * S], U32)
+        x_scales = sb("x_scales", [P, PASSES * S], U8)
+        down_codes = [sb("down_codes%d" % a, [P, R], U32) for a in range(PASSES)]
+        down_scales = [sb("down_scales%d" % a, [P, R], U8) for a in range(PASSES)]
+        h_codes = sb("h_codes", [P, S], U32)
+        h_scales = sb("h_scales", [P, S], U8)
+        up_codes = sb("up_codes", [P, M], U32)
+        up_scales = sb("up_scales", [P, M], U8)
+        head_cols = EARLY * P
+        w4_head = sb("w4_head", [P, PASSES, 2 * head_cols], U8)
+        w4_rest = sb("w4_rest", [P, PASSES, 2 * (M - head_cols)], U8)
+        w4_plane = sb("w4_plane", [P, PASSES, M], U8)
+        b_rows = sb("b_rows", [P, P], F32)
+        ident = sb("ident", [P, P], F32)
+        bias = sb("bias", [P, M // P], F32)
+        h_banks = [psum.tile([P, BANK], F32, name="h_bank%d" % i) for i in range(4)]
+        y_banks = [psum.tile([P, BANK], F32, name="y_bank%d" % i) for i in range(4)]
+
+        nc.gpsimd.memset(w4_plane[:].rearrange("p a n -> p (a n)").bitcast(U32), 0)
+        nc.gpsimd.memset(b_rows[:], 0.0)
+        warm = sb("warm", [P, 8], F32)
+        nc.scalar.activation(warm[:, 0:1], b_rows[:, 0:1], SILU)
+        for page in pages:
+            nc.vector.memset(page[:, 0:1025], 0.0)
+            nc.vector.memset(page[:, 1025:2176], 0.0)
+            nc.gpsimd.memset(page[:, 2176:T], 0.0)
+        make_identity(nc, ident[:])
+
+        def by_word(rows):
+            return rows.rearrange("(p t) c -> p t c", t=PACK)
+
+        def load_x(r, a):
+            nc.sync.dma_start(slots(x_raw[r, a]), by_word(x[a * K_PASS : (a + 1) * K_PASS, r * W : (r + 1) * W]))
+
+        def load_up(i):
+            n0, n1 = UP_PARTS[i]
+            nc.sync.dma_start(slots(up_raw[i]), by_word(up[:, n0:n1]))
+
+        w4_by_part = w4_words.rearrange("a p c -> p a c")
+        for a in range(PASSES):
+            nc.sync.dma_start(slots(down_raw[a]), by_word(down[a * K_PASS : (a + 1) * K_PASS, :]))
+            load_x(0, a)
+        load_up(0)
+        nc.sync.dma_start(w4_head[:].bitcast(I32), w4_by_part[:, :, 0 : 2 * head_cols].bitcast(I32))
+        for q in range(4):
+            nc.sync.dma_start(
+                w4_plane[32 * q : 32 * q + 4, :, :].bitcast(I32),
+                w4_scales[:, 4 * q : 4 * q + 4, :].rearrange("a r n -> r a n").bitcast(I32),
+            )
+        nc.sync.dma_start(b_rows[0 : M // P, :], b.rearrange("(c q) -> c q", q=P))
+        load_x(1, 0)
+        load_up(1)
+        nc.sync.dma_start(lists[:], offs)
+        nc.sync.dma_start(weights[:, 0 : 2 * W], wgo[:, 0 : 2 * W])
+        load_x(1, 1)
+        for r in range(2, ROUNDS - 2):
+            if r == 4:
+                nc.sync.dma_start(weights[:, 2 * W : S], wgo[:, 2 * W : S])
+            load_x(r, 0)
+            load_x(r, 1)
+
+        nc.tensor.transpose(y_banks[3][:, 0:P], b_rows[:], ident[:])
+        nc.scalar.copy(bias[:], y_banks[3][:, 0 : M // P])
+
+        def copy_on(engine, dst, src):
+            if engine == "vector":
+                nc.vector.tensor_copy(dst, src)
+            else:
+                nc.scalar.copy(dst, src)
+
+        def quantise(src, codes, scales):
+            nc.vector.quantize_mx(out=codes.bitcast(FP8X4), scales=scales, in_=src)
+
+        def weave(engine, dst, raw):
+            copy_on(
+                engine,
+                dst.rearrange("p (c i t) -> p c t i", i=4, t=PACK),
+                raw.rearrange("p (t c i) -> p c t i", i=4, t=PACK),
+            )
+
+        def prepare_down(a, engine):
+            copy_on(
+                engine,
+                down_stage[a][:].rearrange("p (u m t) -> p m t u", u=PACK, t=PACK),
+                down_raw[a].rearrange("p (t m u) -> p m t u", u=PACK, t=PACK),
+            )
+            quantise(down_stage[a][:], down_codes[a][:], down_scales[a][:])
+
+        def x_cols(a, c0, width):
+            first = (c0 // W * PASSES + a) * W + c0 % W
+            return slice(first, first + width)
+
+        def weave_x(r, a, engine):
+            weave(engine, stage[r % 2][:, a * PACK * W : (a + 1) * PACK * W], x_raw[r, a])
+
+        def quantise_x(r, a0, a1):
+            cols = x_cols(a0, r * W, (a1 - a0) * W)
+            quantise(stage[r % 2][:, a0 * PACK * W : a1 * PACK * W], x_codes[:, cols], x_scales[:, cols])
+
+        def prepare_early_up(i, engine):
+            n0, n1 = UP_PARTS[i]
+            dst = up_stage[:, PACK * n0 : PACK * n1]
+            weave(engine, dst, up_raw[i])
+            quantise(dst, up_codes[:, n0:n1], up_scales[:, n0:n1])
+
+        def make_h(r):
+            tile = h_stage[r % 2]
+            for c0 in range(r * W, (r + 1) * W, P):
+                bank = h_banks[c0 // P % 4]
+                for a in range(PASSES):
+                    cols = x_cols(a, c0, P)
+                    for u in range(PACK):
+                        nc.tensor.matmul_mx(
+                            out=bank[:, u * P : (u + 1) * P],
+                            lhsT=down_codes[a][:, u * P : (u + 1) * P].bitcast(FP8X4),
+                            lhsT_scale=down_scales[a][:, u * P : (u + 1) * P],
+                            rhs=x_codes[:, cols].bitcast(FP8X4),
+                            rhs_scale=x_scales[:, cols],
+                            start=(a == 0 and u == 0),
+                            stop=(a == PASSES - 1 and u == PACK - 1),
+                        )
+                dst = tile[:, PACK * (c0 % W) : PACK * (c0 % W + P)]
+                copy_on(
+                    "vector" if c0 == P else "scalar",
+                    dst.rearrange("p (c u) -> p c u", u=PACK),
+                    bank[:].rearrange("p (u c) -> p c u", u=PACK),
+                )
+            cols = slice(r * W, (r + 1) * W)
+            quantise(tile[:], h_codes[:, cols], h_scales[:, cols])
+
+        def make_act(n, j0, j1, bank, dst):
+            n0 = n * P
+            w4_tile, first = (w4_head, n0) if n0 < head_cols else (w4_rest, n0 - head_cols)
+            for a in range(PASSES):
+                for c0 in range(j0, j1, P):
+                    cols = x_cols(a, c0, P)
+                    nc.tensor.matmul_mx(
+                        out=bank[:, c0 - j0 : c0 - j0 + P],
+                        lhsT=w4_tile[:, a, 2 * first : 2 * (first + P)].bitcast(FP4X4),
+                        lhsT_scale=w4_plane[:, a, n0 : n0 + P],
+                        rhs=x_codes[:, cols].bitcast(FP8X4),
+                        rhs_scale=x_scales[:, cols],
+                        start=(a == 0 and c0 == j0),
+                        stop=False,
+                    )
+            nc.tensor.matmul_mx(
+                out=bank[:, 0 : j1 - j0],
+                lhsT=up_codes[:, n0 : n0 + P].bitcast(FP8X4),
+                lhsT_scale=up_scales[:, n0 : n0 + P],
+                rhs=h_codes[:, j0:j1].bitcast(FP8X4),
+                rhs_scale=h_scales[:, j0:j1],
+                start=False,
+                stop=True,
+            )
+            nc.scalar.activation(dst, bank[:, 0 : j1 - j0], SILU, bias=bias[:, n : n + 1])
+
+        def place(page, j0, j1, src):
+            nc.vector.tensor_tensor(
+                page[:].indirect(lists[:, j0 // LIST_ROWS : j1 // LIST_ROWS]), src, weights[:, j0:j1], MULT
+            )
+
+        def store(n, page):
+            nc.sync.dma_start(out[n * P : (n + 1) * P, :], page[:])
+
+        prepare_down(0, "scalar")
+        weave_x(0, 0, "scalar")
+        quantise_x(0, 0, 1)
+        prepare_down(1, "vector")
+        weave_x(0, 1, "scalar")
+        quantise_x(0, 1, 2)
+        prepare_early_up(0, "scalar")
+        for r in range(ROUNDS - 2, ROUNDS):
+            load_x(r, 0)
+            load_x(r, 1)
+        nc.sync.dma_start(w4_rest[:].bitcast(I32), w4_by_part[:, :, 2 * head_cols : 2 * M].bitcast(I32))
+        for i in range(2, len(UP_PARTS)):
+            load_up(i)
+        make_h(0)
+        weave_x(1, 0, "vector")
+        quantise_x(1, 0, 1)
+        prepare_early_up(1, "vector")
+
+        def ahead(r, half):
+            if r < ROUNDS:
+                weave_x(r, half, "scalar")
+                if half == 1:
+                    quantise_x(r, 0, PASSES)
+            elif r == ROUNDS:
+                weave("scalar", stage[r % 2][:, half * PACK * W : (half + 1) * PACK * W], up_raw[2 + half])
+                if half == 1:
+                    cols = slice(UP_PARTS[2][0], UP_PARTS[3][1])
+                    quantise(stage[r % 2][:], up_codes[:, cols], up_scales[:, cols])
+            elif half == 0:
+                n0, n1 = UP_PARTS[4]
+                dst = stage[r % 2][:, 0 : PACK * (n1 - n0)]
+                weave("scalar", dst, up_raw[4])
+                quantise(dst, up_codes[:, n0:n1], up_scales[:, n0:n1])
+
+        for r in range(ROUNDS):
+            j0, j1 = r * W, (r + 1) * W
+            behind = x_raw[r + 1, 1][:, 0:W] if r + 1 < ROUNDS else up_raw[3][:, 0:W]
+            free = acts[0][:, j0:j1]
+            held = [free, behind] if r == 0 else [behind, free]
+            make_act(0, j0, j1, y_banks[r % 2], held[0])
+            place(pages[0], j0, j1, held[0])
+            if r == 0:
+                weave_x(1, 1, "scalar")
+                quantise_x(1, 1, 2)
+            if r == ROUNDS - 1:
+                store(0, pages[0])
+            make_act(1, j0, j1, y_banks[2 + r % 2], held[1])
+            place(pages[1], j0, j1, held[1])
+            ahead(r + 2, 0)
+            if r + 1 < ROUNDS:
+                make_h(r + 1)
+            else:
+                store(1, pages[1])
+            make_act(2, j0, j1, h_banks[j1 // P % 4], acts[1][:, j0:j1])
+            place(pages[2], j0, j1, acts[1][:, j0:j1])
+            ahead(r + 2, 1)
+        store(2, pages[2])
+
+        last_page = keep.tile([P, T], F32, name="last_page", tag="shared", align_bytes=64)
+        for c0 in range(0, T, BANK):
+            nc.gpsimd.memset(last_page[:, c0 : c0 + BANK], 0.0)
+        ring = [last_page] + pages
+        for n in range(EARLY, M // P):
+            act = acts[(n - EARLY) % 2]
+            page = ring[(n - EARLY) % len(ring)]
+            for q in range(S // BANK):
+                make_act(n, q * BANK, (q + 1) * BANK, y_banks[q], act[:, q * BANK : (q + 1) * BANK])
+            place(page, 0, S, act[:])
+            store(n, page)

@@ -45,12 +45,16 @@ def tile_list_hscat_l_silu_kernel(tc, x, w4_words, w4_scales, down, up, b, wgo, 
         pages = [sb("page%d" % i, [P, T], F32) for i in range(EARLY)]
         acts = [sb("act%d" % i, [P, S], F32) for i in range(2)]
         weights = sb("weights", [P, S], F32)
-        shared = keep.tile([P, T], F32, name="shared", tag="shared", align_bytes=64)
+        shared = sb("shared", [P, T], F32)
+        first_x = keep.tile([P, T], F32, name="first_x", tag="last_page", align_bytes=64)
         down_raw = [shared[:, a * PACK * R : (a + 1) * PACK * R] for a in range(PASSES)]
         x_raw = {}
         for r in range(ROUNDS):
             for a in range(PASSES):
-                if r < ROUNDS - 2:
+                if r < 2:
+                    first = (PASSES * r + a) * PACK * W
+                    x_raw[r, a] = first_x[:, first : first + PACK * W]
+                elif r < ROUNDS - 2:
                     x_raw[r, a] = sb("x_raw%d_%d" % (r, a), [P, PACK * W], F32)[:]
                 else:
                     first = (PASSES * (r - ROUNDS + 2) + a) * PACK * W
@@ -58,7 +62,7 @@ def tile_list_hscat_l_silu_kernel(tc, x, w4_words, w4_scales, down, up, b, wgo, 
         up_raw = [sb("up_raw%d" % i, [P, PACK * (n1 - n0)], F32)[:] for i, (n0, n1) in enumerate(UP_PARTS)]
         stage = [sb("stage%d" % i, [P, PASSES * PACK * W], BF16) for i in range(2)]
         down_stage = [sb("down_stage%d" % a, [P, PACK * R], BF16) for a in range(PASSES)]
-        up_stage = sb("up_stage", [P, PACK * EARLY * P], BF16)
+        up_stage = sb("up_stage", [P, 2 * PACK * P], BF16)
         h_stage = [sb("h_stage%d" % i, [P, PACK * W], BF16) for i in range(2)]
         x_codes = sb("x_codes", [P, PASSES * S], U32)
         x_scales = sb("x_scales", [P, PASSES * S], U8)
@@ -71,21 +75,22 @@ def tile_list_hscat_l_silu_kernel(tc, x, w4_words, w4_scales, down, up, b, wgo, 
         head_cols = EARLY * P
         w4_head = sb("w4_head", [P, PASSES, 2 * head_cols], U8)
         w4_rest = sb("w4_rest", [P, PASSES, 2 * (M - head_cols)], U8)
-        w4_plane = sb("w4_plane", [P, PASSES, M], U8)
+        plane_head = sb("plane_head", [P, PASSES, head_cols], U8)
+        plane_rest = sb("plane_rest", [P, PASSES, M - head_cols], U8)
         b_rows = sb("b_rows", [P, P], F32)
         ident = sb("ident", [P, P], F32)
         bias = sb("bias", [P, M // P], F32)
         h_banks = [psum.tile([P, BANK], F32, name="h_bank%d" % i) for i in range(4)]
         y_banks = [psum.tile([P, BANK], F32, name="y_bank%d" % i) for i in range(4)]
 
-        nc.gpsimd.memset(w4_plane[:].rearrange("p a n -> p (a n)").bitcast(U32), 0)
+        nc.gpsimd.memset(plane_head[:].rearrange("p a n -> p (a n)").bitcast(U32), 0)
         nc.gpsimd.memset(b_rows[:], 0.0)
         warm = sb("warm", [P, 8], F32)
-        nc.scalar.activation(warm[:, 0:1], b_rows[:, 0:1], SILU)
+        nc.vector.memset(warm[:], 0.0)
+        nc.scalar.activation(warm[:, 0:1], warm[:, 4:5], SILU)
+        nc.vector.memset(plane_rest[:].rearrange("p a n -> p (a n)").bitcast(U32), 0)
         for page in pages:
-            nc.vector.memset(page[:, 0:1025], 0.0)
-            nc.vector.memset(page[:, 1025:2176], 0.0)
-            nc.gpsimd.memset(page[:, 2176:T], 0.0)
+            nc.vector.memset(page[:], 0.0)
         make_identity(nc, ident[:])
 
         def by_word(rows):
@@ -99,27 +104,35 @@ def tile_list_hscat_l_silu_kernel(tc, x, w4_words, w4_scales, down, up, b, wgo, 
             nc.sync.dma_start(slots(up_raw[i]), by_word(up[:, n0:n1]))
 
         w4_by_part = w4_words.rearrange("a p c -> p a c")
-        for a in range(PASSES):
+
+        def load_down(a):
             nc.sync.dma_start(slots(down_raw[a]), by_word(down[a * K_PASS : (a + 1) * K_PASS, :]))
-            load_x(0, a)
+
+        def load_plane(plane, n0, n1):
+            for q in range(4):
+                nc.sync.dma_start(
+                    plane[32 * q : 32 * q + 4, :, :].bitcast(I32),
+                    w4_scales[:, 4 * q : 4 * q + 4, n0:n1].rearrange("a r n -> r a n").bitcast(I32),
+                )
+
+        load_down(0)
+        nc.sync.dma_start(b_rows[0 : M // P, :], b.rearrange("(c q) -> c q", q=P))
+        load_plane(plane_head, 0, head_cols)
+        nc.sync.dma_start(lists[:], offs)
+        load_x(0, 0)
+        load_down(1)
+        load_x(0, 1)
+        load_x(1, 0)
         load_up(0)
         nc.sync.dma_start(w4_head[:].bitcast(I32), w4_by_part[:, :, 0 : 2 * head_cols].bitcast(I32))
-        for q in range(4):
-            nc.sync.dma_start(
-                w4_plane[32 * q : 32 * q + 4, :, :].bitcast(I32),
-                w4_scales[:, 4 * q : 4 * q + 4, :].rearrange("a r n -> r a n").bitcast(I32),
-            )
-        nc.sync.dma_start(b_rows[0 : M // P, :], b.rearrange("(c q) -> c q", q=P))
-        load_x(1, 0)
-        load_up(1)
-        nc.sync.dma_start(lists[:], offs)
-        nc.sync.dma_start(weights[:, 0 : 2 * W], wgo[:, 0 : 2 * W])
         load_x(1, 1)
+        nc.sync.dma_start(weights[:, 0 : 2 * W], wgo[:, 0 : 2 * W])
+        load_up(1)
         for r in range(2, ROUNDS - 2):
-            if r == 4:
-                nc.sync.dma_start(weights[:, 2 * W : S], wgo[:, 2 * W : S])
             load_x(r, 0)
             load_x(r, 1)
+            if r == 3:
+                nc.sync.dma_start(weights[:, 2 * W : S], wgo[:, 2 * W : S])
 
         nc.tensor.transpose(y_banks[3][:, 0:P], b_rows[:], ident[:])
         nc.scalar.copy(bias[:], y_banks[3][:, 0 : M // P])
@@ -133,40 +146,51 @@ def tile_list_hscat_l_silu_kernel(tc, x, w4_words, w4_scales, down, up, b, wgo, 
         def quantise(src, codes, scales):
             nc.vector.quantize_mx(out=codes.bitcast(FP8X4), scales=scales, in_=src)
 
-        def weave(engine, dst, raw):
+        def weave(engine, dst, raw, c0, c1):
             copy_on(
                 engine,
-                dst.rearrange("p (c i t) -> p c t i", i=4, t=PACK),
-                raw.rearrange("p (t c i) -> p c t i", i=4, t=PACK),
+                dst[:, PACK * c0 : PACK * c1].rearrange("p (c i t) -> p c t i", i=4, t=PACK),
+                slots(raw)[:, :, c0:c1].rearrange("p t (c i) -> p c t i", i=4),
             )
 
-        def prepare_down(a, engine):
+        def weave_down(engine, a, m0, m1):
             copy_on(
                 engine,
-                down_stage[a][:].rearrange("p (u m t) -> p m t u", u=PACK, t=PACK),
-                down_raw[a].rearrange("p (t m u) -> p m t u", u=PACK, t=PACK),
+                down_stage[a][:].rearrange("p (u m t) -> p m t u", u=PACK, t=PACK)[:, m0:m1],
+                down_raw[a].rearrange("p (t m u) -> p m t u", u=PACK, t=PACK)[:, m0:m1],
             )
+
+        def quantise_down(a):
             quantise(down_stage[a][:], down_codes[a][:], down_scales[a][:])
 
         def x_cols(a, c0, width):
             first = (c0 // W * PASSES + a) * W + c0 % W
             return slice(first, first + width)
 
-        def weave_x(r, a, engine):
-            weave(engine, stage[r % 2][:, a * PACK * W : (a + 1) * PACK * W], x_raw[r, a])
+        def weave_x(engine, r, a, c0, c1):
+            weave(engine, stage[r % 2][:, a * PACK * W : (a + 1) * PACK * W], x_raw[r, a], c0, c1)
 
-        def quantise_x(r, a0, a1):
-            cols = x_cols(a0, r * W, (a1 - a0) * W)
-            quantise(stage[r % 2][:, a0 * PACK * W : a1 * PACK * W], x_codes[:, cols], x_scales[:, cols])
+        def quantise_x(r, c0, c1):
+            cols = slice(r * PASSES * W + c0, r * PASSES * W + c1)
+            quantise(stage[r % 2][:, PACK * c0 : PACK * c1], x_codes[:, cols], x_scales[:, cols])
 
-        def prepare_early_up(i, engine):
-            n0, n1 = UP_PARTS[i]
-            dst = up_stage[:, PACK * n0 : PACK * n1]
-            weave(engine, dst, up_raw[i])
-            quantise(dst, up_codes[:, n0:n1], up_scales[:, n0:n1])
+        half = PACK * W
+        middle = [tile[:, half // 2 : half // 2 + half] for tile in stage]
+
+        def weave_early_up(engine, n, dst):
+            i = 0 if n * P < UP_PARTS[0][1] else 1
+            first = n * P - UP_PARTS[i][0]
+            copy_on(
+                engine,
+                dst.rearrange("p (c i t) -> p c t i", i=4, t=PACK),
+                slots(up_raw[i])[:, :, first : first + P].rearrange("p t (c i) -> p c t i", i=4),
+            )
+
+        def quantise_early_up(n, src):
+            quantise(src, up_codes[:, n * P : (n + 1) * P], up_scales[:, n * P : (n + 1) * P])
 
         def make_h(r):
-            tile = h_stage[r % 2]
+            tile = middle[r] if r < 2 else h_stage[r % 2][:]
             for c0 in range(r * W, (r + 1) * W, P):
                 bank = h_banks[c0 // P % 4]
                 for a in range(PASSES):
@@ -188,18 +212,19 @@ def tile_list_hscat_l_silu_kernel(tc, x, w4_words, w4_scales, down, up, b, wgo, 
                     bank[:].rearrange("p (u c) -> p c u", u=PACK),
                 )
             cols = slice(r * W, (r + 1) * W)
-            quantise(tile[:], h_codes[:, cols], h_scales[:, cols])
+            quantise(tile, h_codes[:, cols], h_scales[:, cols])
 
-        def make_act(n, j0, j1, bank, dst):
+        def make_y(n, j0, j1, bank):
             n0 = n * P
-            w4_tile, first = (w4_head, n0) if n0 < head_cols else (w4_rest, n0 - head_cols)
+            early = n0 < head_cols
+            w4_tile, plane, first = (w4_head, plane_head, n0) if early else (w4_rest, plane_rest, n0 - head_cols)
             for a in range(PASSES):
                 for c0 in range(j0, j1, P):
                     cols = x_cols(a, c0, P)
                     nc.tensor.matmul_mx(
                         out=bank[:, c0 - j0 : c0 - j0 + P],
                         lhsT=w4_tile[:, a, 2 * first : 2 * (first + P)].bitcast(FP4X4),
-                        lhsT_scale=w4_plane[:, a, n0 : n0 + P],
+                        lhsT_scale=plane[:, a, first : first + P],
                         rhs=x_codes[:, cols].bitcast(FP8X4),
                         rhs_scale=x_scales[:, cols],
                         start=(a == 0 and c0 == j0),
@@ -214,7 +239,9 @@ def tile_list_hscat_l_silu_kernel(tc, x, w4_words, w4_scales, down, up, b, wgo, 
                 start=False,
                 stop=True,
             )
-            nc.scalar.activation(dst, bank[:, 0 : j1 - j0], SILU, bias=bias[:, n : n + 1])
+
+        def activate(n, src, dst):
+            nc.scalar.activation(dst, src, SILU, bias=bias[:, n : n + 1])
 
         def place(page, j0, j1, src):
             nc.vector.tensor_tensor(
@@ -224,72 +251,81 @@ def tile_list_hscat_l_silu_kernel(tc, x, w4_words, w4_scales, down, up, b, wgo, 
         def store(n, page):
             nc.sync.dma_start(out[n * P : (n + 1) * P, :], page[:])
 
-        prepare_down(0, "scalar")
-        weave_x(0, 0, "scalar")
-        quantise_x(0, 0, 1)
-        prepare_down(1, "vector")
-        weave_x(0, 1, "scalar")
-        quantise_x(0, 1, 2)
-        prepare_early_up(0, "scalar")
+        weave_down("scalar", 0, 0, P)
+        quantise_down(0)
+        weave_x("scalar", 0, 0, 0, W)
+        weave_down("vector", 1, 0, 96)
+        weave_down("scalar", 1, 96, P)
+        quantise_x(0, 0, W)
+        quantise_down(1)
+        weave_x("scalar", 0, 1, 0, P)
+        quantise_x(0, W, W + P)
+        weave_x("vector", 0, 1, P, W)
+        quantise_x(0, W + P, 2 * W)
+        weave_x("vector", 1, 0, 0, W)
+        quantise_x(1, 0, W)
+        weave_early_up("vector", 0, up_stage[:, 0 : PACK * P])
+        quantise_early_up(0, up_stage[:, 0 : PACK * P])
         for r in range(ROUNDS - 2, ROUNDS):
             load_x(r, 0)
             load_x(r, 1)
         nc.sync.dma_start(w4_rest[:].bitcast(I32), w4_by_part[:, :, 2 * head_cols : 2 * M].bitcast(I32))
         for i in range(2, len(UP_PARTS)):
             load_up(i)
+        load_plane(plane_rest, head_cols, M)
         make_h(0)
-        weave_x(1, 0, "vector")
-        quantise_x(1, 0, 1)
-        prepare_early_up(1, "vector")
+        weave_early_up("vector", 1, up_stage[:, PACK * P :])
+        quantise_early_up(1, up_stage[:, PACK * P :])
+        weave("vector", middle[0], x_raw[1, 1], 0, W)
+        quantise(middle[0], x_codes[:, x_cols(1, W, W)], x_scales[:, x_cols(1, W, W)])
+        weave_early_up("vector", 2, middle[0][:, 0 : PACK * P])
+        quantise_early_up(2, middle[0][:, 0 : PACK * P])
 
-        def ahead(r, half):
+        def ahead(r, a):
             if r < ROUNDS:
-                weave_x(r, half, "scalar")
-                if half == 1:
-                    quantise_x(r, 0, PASSES)
+                weave_x("scalar", r, a, 0, W)
+                if a == 1:
+                    quantise_x(r, 0, PASSES * W)
             elif r == ROUNDS:
-                weave("scalar", stage[r % 2][:, half * PACK * W : (half + 1) * PACK * W], up_raw[2 + half])
-                if half == 1:
+                weave("scalar", stage[r % 2][:, a * half :], up_raw[2 + a], 0, W)
+                if a == 1:
                     cols = slice(UP_PARTS[2][0], UP_PARTS[3][1])
                     quantise(stage[r % 2][:], up_codes[:, cols], up_scales[:, cols])
-            elif half == 0:
+            elif a == 1:
                 n0, n1 = UP_PARTS[4]
-                dst = stage[r % 2][:, 0 : PACK * (n1 - n0)]
-                weave("scalar", dst, up_raw[4])
-                quantise(dst, up_codes[:, n0:n1], up_scales[:, n0:n1])
+                weave("scalar", stage[r % 2][:], up_raw[4], 0, n1 - n0)
+                quantise(stage[r % 2][:, 0 : PACK * (n1 - n0)], up_codes[:, n0:n1], up_scales[:, n0:n1])
 
+        second_halves = [x_raw[r, 1] for r in range(1, ROUNDS)] + [up_raw[3]]
         for r in range(ROUNDS):
             j0, j1 = r * W, (r + 1) * W
-            behind = x_raw[r + 1, 1][:, 0:W] if r + 1 < ROUNDS else up_raw[3][:, 0:W]
-            free = acts[0][:, j0:j1]
-            held = [free, behind] if r == 0 else [behind, free]
-            make_act(0, j0, j1, y_banks[r % 2], held[0])
-            place(pages[0], j0, j1, held[0])
-            if r == 0:
-                weave_x(1, 1, "scalar")
-                quantise_x(1, 1, 2)
-            if r == ROUNDS - 1:
-                store(0, pages[0])
-            make_act(1, j0, j1, y_banks[2 + r % 2], held[1])
-            place(pages[1], j0, j1, held[1])
+            for n in range(2):
+                bank = h_banks[n] if r == 0 else y_banks[n]
+                held = acts[0][:, 0:W] if r == 0 and n == 0 else second_halves[r][:, n * W : (n + 1) * W]
+                make_y(n, j0, j1, bank[:, 0:W])
+                activate(n, bank[:, 0:W], held)
+                place(pages[n], j0, j1, held)
+                if r == ROUNDS - 1:
+                    store(n, pages[n])
             ahead(r + 2, 0)
             if r + 1 < ROUNDS:
                 make_h(r + 1)
-            else:
-                store(1, pages[1])
-            make_act(2, j0, j1, h_banks[j1 // P % 4], acts[1][:, j0:j1])
+            bank = h_banks[j1 // P % 4]
+            make_y(2, j0, j1, bank[:, 0:W])
+            activate(2, bank[:, 0:W], acts[1][:, j0:j1])
             place(pages[2], j0, j1, acts[1][:, j0:j1])
             ahead(r + 2, 1)
         store(2, pages[2])
 
-        last_page = keep.tile([P, T], F32, name="last_page", tag="shared", align_bytes=64)
-        for c0 in range(0, T, BANK):
-            nc.gpsimd.memset(last_page[:, c0 : c0 + BANK], 0.0)
+        last_page = keep.tile([P, T], F32, name="last_page", tag="last_page", align_bytes=64)
+        for c0 in range(0, T, W):
+            nc.gpsimd.memset(last_page[:, c0 : c0 + W], 0.0)
         ring = [last_page] + pages
         for n in range(EARLY, M // P):
             act = acts[(n - EARLY) % 2]
             page = ring[(n - EARLY) % len(ring)]
             for q in range(S // BANK):
-                make_act(n, q * BANK, (q + 1) * BANK, y_banks[q], act[:, q * BANK : (q + 1) * BANK])
+                make_y(n, q * BANK, (q + 1) * BANK, y_banks[q][:])
+                activate(n, y_banks[q][:], act[:, q * BANK : (q + 1) * BANK])
             place(page, 0, S, act[:])
             store(n, page)

@@ -90,7 +90,7 @@ def tile_list_hscat_l_silu_kernel(tc, x, w4_words, w4_scales, down, up, b, wgo, 
         nc.scalar.activation(warm[:, 0:1], warm[:, 4:5], SILU)
         nc.vector.memset(plane_rest[:].rearrange("p a n -> p (a n)").bitcast(U32), 0)
         for page in pages:
-            nc.vector.memset(page[:], 0.0)
+            nc.vector.memset(page[:].bitcast(U32), 0)
         make_identity(nc, ident[:])
 
         def by_word(rows):
@@ -278,8 +278,8 @@ def tile_list_hscat_l_silu_kernel(tc, x, w4_words, w4_scales, down, up, b, wgo, 
         quantise_early_up(1, up_stage[:, PACK * P :])
         weave("vector", middle[0], x_raw[1, 1], 0, W)
         quantise(middle[0], x_codes[:, x_cols(1, W, W)], x_scales[:, x_cols(1, W, W)])
-        weave_early_up("vector", 2, middle[0][:, 0 : PACK * P])
-        quantise_early_up(2, middle[0][:, 0 : PACK * P])
+        weave_early_up("vector", 2, middle[0][:, PACK * P :])
+        quantise_early_up(2, middle[0][:, PACK * P :])
 
         def ahead(r, a):
             if r < ROUNDS:
@@ -319,7 +319,7 @@ def tile_list_hscat_l_silu_kernel(tc, x, w4_words, w4_scales, down, up, b, wgo, 
 
         last_page = keep.tile([P, T], F32, name="last_page", tag="last_page", align_bytes=64)
         for c0 in range(0, T, W):
-            nc.gpsimd.memset(last_page[:, c0 : c0 + W], 0.0)
+            nc.gpsimd.memset(last_page[:, c0 : c0 + W].bitcast(U32), 0)
         ring = [last_page] + pages
         for n in range(EARLY, M // P):
             act = acts[(n - EARLY) % 2]

@@ -15,6 +15,7 @@ U8 = mybir.dt.uint8
 FP8X4 = mybir.dt.float8_e4m3fn_x4
 FP4X4 = mybir.dt.float4_e2m1fn_x4
 SILU = mybir.ActivationFunctionType.Silu
+IDENTITY = mybir.ActivationFunctionType.Identity
 MULT = mybir.AluOpType.mult
 
 P = 128
@@ -22,11 +23,16 @@ PACK = 4
 K_PASS = P * PACK
 PASSES = K // K_PASS
 BANK = 512
+QUADRANTS = 4
 LIST_ROWS = 16
+LINE = 4
 W = 256
 ROUNDS = S // W
+HALF = PACK * W
 EARLY = 3
+EARLY_COLS = EARLY * P
 UP_PARTS = [(0, 256), (256, 384), (384, 640), (640, 896), (896, 1024)]
+DOWN_ON_VECTOR = 96
 
 
 def tile_list_hscat_l_silu_kernel(tc, x, w4_words, w4_scales, down, up, b, wgo, offs, out):
@@ -35,66 +41,64 @@ def tile_list_hscat_l_silu_kernel(tc, x, w4_words, w4_scales, down, up, b, wgo, 
         keep = ctx.enter_context(tc.tile_pool(name="keep", bufs=1))
         psum = ctx.enter_context(tc.psum_pool(name="psum", bufs=1))
 
-        def sb(name, shape, dtype):
+        def sbuf(name, shape, dtype):
             return keep.tile(shape, dtype, name=name, align_bytes=64)
 
         def slots(ap):
             return ap.rearrange("p (t c) -> p t c", t=PACK)
 
         lists = keep.tile([P, S // LIST_ROWS], U16, name="lists")
-        pages = [sb("page%d" % i, [P, T], F32) for i in range(EARLY)]
-        acts = [sb("act%d" % i, [P, S], F32) for i in range(2)]
-        weights = sb("weights", [P, S], F32)
-        shared = sb("shared", [P, T], F32)
-        first_x = keep.tile([P, T], F32, name="first_x", tag="last_page", align_bytes=64)
-        down_raw = [shared[:, a * PACK * R : (a + 1) * PACK * R] for a in range(PASSES)]
+        pages = [sbuf("page%d" % i, [P, T], F32) for i in range(2)]
+        acts = [sbuf("act%d" % i, [P, S], F32) for i in range(2)]
+        weights = sbuf("weights", [P, S], F32)
+        down_then_x = sbuf("down_then_x", [P, T], F32)
+        x_pairs = [keep.tile([P, T], F32, name="x_pair%d" % i, tag="late%d" % i, align_bytes=64) for i in range(2)]
+        down_raw = [down_then_x[:, a * PACK * R : (a + 1) * PACK * R] for a in range(PASSES)]
         x_raw = {}
         for r in range(ROUNDS):
             for a in range(PASSES):
-                if r < 2:
-                    first = (PASSES * r + a) * PACK * W
-                    x_raw[r, a] = first_x[:, first : first + PACK * W]
+                first = (PASSES * (r % 2) + a) * HALF
+                if r < 2 * len(x_pairs):
+                    x_raw[r, a] = x_pairs[r // 2][:, first : first + HALF]
                 elif r < ROUNDS - 2:
-                    x_raw[r, a] = sb("x_raw%d_%d" % (r, a), [P, PACK * W], F32)[:]
+                    x_raw[r, a] = sbuf("x_raw%d_%d" % (r, a), [P, HALF], F32)[:]
                 else:
-                    first = (PASSES * (r - ROUNDS + 2) + a) * PACK * W
-                    x_raw[r, a] = shared[:, first : first + PACK * W]
-        up_raw = [sb("up_raw%d" % i, [P, PACK * (n1 - n0)], F32)[:] for i, (n0, n1) in enumerate(UP_PARTS)]
-        stage = [sb("stage%d" % i, [P, PASSES * PACK * W], BF16) for i in range(2)]
-        down_stage = [sb("down_stage%d" % a, [P, PACK * R], BF16) for a in range(PASSES)]
-        up_stage = sb("up_stage", [P, 2 * PACK * P], BF16)
-        h_stage = [sb("h_stage%d" % i, [P, PACK * W], BF16) for i in range(2)]
-        x_codes = sb("x_codes", [P, PASSES * S], U32)
-        x_scales = sb("x_scales", [P, PASSES * S], U8)
-        down_codes = [sb("down_codes%d" % a, [P, R], U32) for a in range(PASSES)]
-        down_scales = [sb("down_scales%d" % a, [P, R], U8) for a in range(PASSES)]
-        h_codes = sb("h_codes", [P, S], U32)
-        h_scales = sb("h_scales", [P, S], U8)
-        up_codes = sb("up_codes", [P, M], U32)
-        up_scales = sb("up_scales", [P, M], U8)
-        head_cols = EARLY * P
-        w4_head = sb("w4_head", [P, PASSES, 2 * head_cols], U8)
-        w4_rest = sb("w4_rest", [P, PASSES, 2 * (M - head_cols)], U8)
-        plane_head = sb("plane_head", [P, PASSES, head_cols], U8)
-        plane_rest = sb("plane_rest", [P, PASSES, M - head_cols], U8)
-        b_rows = sb("b_rows", [P, P], F32)
-        ident = sb("ident", [P, P], F32)
-        bias = sb("bias", [P, M // P], F32)
+                    x_raw[r, a] = down_then_x[:, first : first + HALF]
+        up_raw = [sbuf("up_raw%d" % i, [P, PACK * (n1 - n0)], F32)[:] for i, (n0, n1) in enumerate(UP_PARTS)]
+        stage = [sbuf("stage%d" % i, [P, PASSES * HALF], BF16) for i in range(2)]
+        down_stage = [sbuf("down_stage%d" % a, [P, PACK * R], BF16) for a in range(PASSES)]
+        up_stage = sbuf("up_stage", [P, 2 * K_PASS], BF16)
+        h_stage = [sbuf("h_stage%d" % i, [P, HALF], BF16) for i in range(2)]
+        x_codes = sbuf("x_codes", [P, PASSES * S], U32)
+        x_scales = sbuf("x_scales", [P, PASSES * S], U8)
+        down_codes = [sbuf("down_codes%d" % a, [P, R], U32) for a in range(PASSES)]
+        down_scales = [sbuf("down_scales%d" % a, [P, R], U8) for a in range(PASSES)]
+        h_codes = sbuf("h_codes", [P, S], U32)
+        h_scales = sbuf("h_scales", [P, S], U8)
+        up_codes = sbuf("up_codes", [P, M], U32)
+        up_scales = sbuf("up_scales", [P, M], U8)
+        w4_early = sbuf("w4_early", [P, PASSES, 2 * EARLY_COLS], U8)
+        w4_late = sbuf("w4_late", [P, PASSES, 2 * (M - EARLY_COLS)], U8)
+        w4_scales_early = sbuf("w4_scales_early", [P, PASSES, EARLY_COLS], U8)
+        w4_scales_late = sbuf("w4_scales_late", [P, PASSES, M - EARLY_COLS], U8)
+        b_rows = sbuf("b_rows", [P, P], F32)
+        ident = sbuf("ident", [P, P], F32)
+        bias = sbuf("bias", [P, M // P], F32)
         h_banks = [psum.tile([P, BANK], F32, name="h_bank%d" % i) for i in range(4)]
-        y_banks = [psum.tile([P, BANK], F32, name="y_bank%d" % i) for i in range(4)]
+        y_banks = [psum.tile([P, BANK], F32, name="y_bank%d" % i) for i in range(S // BANK)]
 
-        nc.gpsimd.memset(plane_head[:].rearrange("p a n -> p (a n)").bitcast(U32), 0)
+        nc.gpsimd.memset(w4_scales_early[:].rearrange("p a n -> p (a n)").bitcast(U32), 0)
         nc.gpsimd.memset(b_rows[:], 0.0)
-        warm = sb("warm", [P, 8], F32)
-        nc.vector.memset(warm[:], 0.0)
-        nc.scalar.activation(warm[:, 0:1], warm[:, 4:5], SILU)
-        nc.vector.memset(plane_rest[:].rearrange("p a n -> p (a n)").bitcast(U32), 0)
+        nc.vector.memset(w4_scales_late[:].rearrange("p a n -> p (a n)").bitcast(U32), 0)
         for page in pages:
             nc.vector.memset(page[:].bitcast(U32), 0)
         make_identity(nc, ident[:])
 
         def by_word(rows):
             return rows.rearrange("(p t) c -> p t c", t=PACK)
+
+        def load_down(a):
+            nc.sync.dma_start(slots(down_raw[a]), by_word(down[a * K_PASS : (a + 1) * K_PASS, :]))
 
         def load_x(r, a):
             nc.sync.dma_start(slots(x_raw[r, a]), by_word(x[a * K_PASS : (a + 1) * K_PASS, r * W : (r + 1) * W]))
@@ -103,59 +107,55 @@ def tile_list_hscat_l_silu_kernel(tc, x, w4_words, w4_scales, down, up, b, wgo, 
             n0, n1 = UP_PARTS[i]
             nc.sync.dma_start(slots(up_raw[i]), by_word(up[:, n0:n1]))
 
-        w4_by_part = w4_words.rearrange("a p c -> p a c")
+        def load_w4(tile, n0, n1):
+            words = w4_words.rearrange("a p c -> p a c")[:, :, 2 * n0 : 2 * n1]
+            nc.sync.dma_start(tile[:].bitcast(I32), words.bitcast(I32))
 
-        def load_down(a):
-            nc.sync.dma_start(slots(down_raw[a]), by_word(down[a * K_PASS : (a + 1) * K_PASS, :]))
-
-        def load_plane(plane, n0, n1):
-            for q in range(4):
+        def load_w4_scales(tile, n0, n1):
+            for q in range(QUADRANTS):
                 nc.sync.dma_start(
-                    plane[32 * q : 32 * q + 4, :, :].bitcast(I32),
+                    tile[32 * q : 32 * q + 4, :, :].bitcast(I32),
                     w4_scales[:, 4 * q : 4 * q + 4, n0:n1].rearrange("a r n -> r a n").bitcast(I32),
                 )
 
+        def load_weights(j0, j1):
+            nc.sync.dma_start(weights[:, j0:j1], wgo[:, j0:j1])
+
         load_down(0)
         nc.sync.dma_start(b_rows[0 : M // P, :], b.rearrange("(c q) -> c q", q=P))
-        load_plane(plane_head, 0, head_cols)
+        load_w4_scales(w4_scales_early, 0, EARLY_COLS)
         nc.sync.dma_start(lists[:], offs)
         load_x(0, 0)
         load_down(1)
         load_x(0, 1)
         load_x(1, 0)
         load_up(0)
-        nc.sync.dma_start(w4_head[:].bitcast(I32), w4_by_part[:, :, 0 : 2 * head_cols].bitcast(I32))
+        load_w4(w4_early, 0, EARLY_COLS)
         load_x(1, 1)
-        nc.sync.dma_start(weights[:, 0 : 2 * W], wgo[:, 0 : 2 * W])
+        load_weights(0, 2 * W)
         load_up(1)
-        for r in range(2, ROUNDS - 2):
+        for r in (2, 3):
             load_x(r, 0)
             load_x(r, 1)
-            if r == 3:
-                nc.sync.dma_start(weights[:, 2 * W : S], wgo[:, 2 * W : S])
+        load_weights(2 * W, S)
+        for r in range(4, ROUNDS - 2):
+            load_x(r, 0)
+            load_x(r, 1)
 
-        nc.tensor.transpose(y_banks[3][:, 0:P], b_rows[:], ident[:])
-        nc.scalar.copy(bias[:], y_banks[3][:, 0 : M // P])
-
-        def copy_on(engine, dst, src):
-            if engine == "vector":
-                nc.vector.tensor_copy(dst, src)
-            else:
-                nc.scalar.copy(dst, src)
+        nc.tensor.transpose(y_banks[-1][:, 0:P], b_rows[:], ident[:])
+        nc.scalar.copy(bias[:], y_banks[-1][:, 0 : M // P])
 
         def quantise(src, codes, scales):
             nc.vector.quantize_mx(out=codes.bitcast(FP8X4), scales=scales, in_=src)
 
-        def weave(engine, dst, raw, c0, c1):
-            copy_on(
-                engine,
-                dst[:, PACK * c0 : PACK * c1].rearrange("p (c i t) -> p c t i", i=4, t=PACK),
-                slots(raw)[:, :, c0:c1].rearrange("p t (c i) -> p c t i", i=4),
+        def weave(copy, dst, raw, c0, c1):
+            copy(
+                dst.rearrange("p (c i t) -> p c t i", i=LINE, t=PACK),
+                slots(raw)[:, :, c0:c1].rearrange("p t (c i) -> p c t i", i=LINE),
             )
 
-        def weave_down(engine, a, m0, m1):
-            copy_on(
-                engine,
+        def weave_down(copy, a, m0, m1):
+            copy(
                 down_stage[a][:].rearrange("p (u m t) -> p m t u", u=PACK, t=PACK)[:, m0:m1],
                 down_raw[a].rearrange("p (t m u) -> p m t u", u=PACK, t=PACK)[:, m0:m1],
             )
@@ -163,38 +163,38 @@ def tile_list_hscat_l_silu_kernel(tc, x, w4_words, w4_scales, down, up, b, wgo, 
         def quantise_down(a):
             quantise(down_stage[a][:], down_codes[a][:], down_scales[a][:])
 
-        def x_cols(a, c0, width):
-            first = (c0 // W * PASSES + a) * W + c0 % W
+        def x_cols(a, j0, width):
+            first = (j0 // W * PASSES + a) * W + j0 % W
             return slice(first, first + width)
 
-        def weave_x(engine, r, a, c0, c1):
-            weave(engine, stage[r % 2][:, a * PACK * W : (a + 1) * PACK * W], x_raw[r, a], c0, c1)
+        def x_stage(r, a, c0, c1):
+            return stage[r % 2][:, a * HALF + PACK * c0 : a * HALF + PACK * c1]
 
-        def quantise_x(r, c0, c1):
-            cols = slice(r * PASSES * W + c0, r * PASSES * W + c1)
-            quantise(stage[r % 2][:, PACK * c0 : PACK * c1], x_codes[:, cols], x_scales[:, cols])
+        def weave_x(copy, r, a, c0, c1):
+            weave(copy, x_stage(r, a, c0, c1), x_raw[r, a], c0, c1)
 
-        half = PACK * W
-        middle = [tile[:, half // 2 : half // 2 + half] for tile in stage]
+        def quantise_x(src, r, a, c0):
+            cols = x_cols(a, r * W + c0, src.shape[1] // PACK)
+            quantise(src, x_codes[:, cols], x_scales[:, cols])
 
-        def weave_early_up(engine, n, dst):
-            i = 0 if n * P < UP_PARTS[0][1] else 1
-            first = n * P - UP_PARTS[i][0]
-            copy_on(
-                engine,
-                dst.rearrange("p (c i t) -> p c t i", i=4, t=PACK),
-                slots(up_raw[i])[:, :, first : first + P].rearrange("p t (c i) -> p c t i", i=4),
-            )
+        def quantise_up(src, n0):
+            cols = slice(n0, n0 + src.shape[1] // PACK)
+            quantise(src, up_codes[:, cols], up_scales[:, cols])
 
-        def quantise_early_up(n, src):
-            quantise(src, up_codes[:, n * P : (n + 1) * P], up_scales[:, n * P : (n + 1) * P])
+        def prepare_early_up(n, dst):
+            part = 0 if n * P < UP_PARTS[0][1] else 1
+            first = n * P - UP_PARTS[part][0]
+            weave(nc.vector.tensor_copy, dst, up_raw[part], first, first + P)
+            quantise_up(dst, n * P)
+
+        middle = [tile[:, HALF // 2 : HALF // 2 + HALF] for tile in stage]
 
         def make_h(r):
-            tile = middle[r] if r < 2 else h_stage[r % 2][:]
-            for c0 in range(r * W, (r + 1) * W, P):
-                bank = h_banks[c0 // P % 4]
+            tile = middle[r] if r < len(middle) else h_stage[r % 2][:]
+            for j0 in range(r * W, (r + 1) * W, P):
+                bank = h_banks[j0 // P % len(h_banks)]
                 for a in range(PASSES):
-                    cols = x_cols(a, c0, P)
+                    cols = x_cols(a, j0, P)
                     for u in range(PACK):
                         nc.tensor.matmul_mx(
                             out=bank[:, u * P : (u + 1) * P],
@@ -205,29 +205,29 @@ def tile_list_hscat_l_silu_kernel(tc, x, w4_words, w4_scales, down, up, b, wgo, 
                             start=(a == 0 and u == 0),
                             stop=(a == PASSES - 1 and u == PACK - 1),
                         )
-                dst = tile[:, PACK * (c0 % W) : PACK * (c0 % W + P)]
-                copy_on(
-                    "vector" if c0 == P else "scalar",
-                    dst.rearrange("p (c u) -> p c u", u=PACK),
+                copy = nc.vector.tensor_copy if j0 == P else nc.scalar.copy
+                copy(
+                    tile[:, PACK * (j0 % W) : PACK * (j0 % W + P)].rearrange("p (c u) -> p c u", u=PACK),
                     bank[:].rearrange("p (u c) -> p c u", u=PACK),
                 )
-            cols = slice(r * W, (r + 1) * W)
-            quantise(tile, h_codes[:, cols], h_scales[:, cols])
+            quantise(tile, h_codes[:, r * W : (r + 1) * W], h_scales[:, r * W : (r + 1) * W])
 
-        def make_y(n, j0, j1, bank):
+        def make_act(n, j0, j1, bank, dst):
             n0 = n * P
-            early = n0 < head_cols
-            w4_tile, plane, first = (w4_head, plane_head, n0) if early else (w4_rest, plane_rest, n0 - head_cols)
+            if n < EARLY:
+                words, scales, first = w4_early, w4_scales_early, n0
+            else:
+                words, scales, first = w4_late, w4_scales_late, n0 - EARLY_COLS
             for a in range(PASSES):
-                for c0 in range(j0, j1, P):
-                    cols = x_cols(a, c0, P)
+                for j in range(j0, j1, P):
+                    cols = x_cols(a, j, P)
                     nc.tensor.matmul_mx(
-                        out=bank[:, c0 - j0 : c0 - j0 + P],
-                        lhsT=w4_tile[:, a, 2 * first : 2 * (first + P)].bitcast(FP4X4),
-                        lhsT_scale=plane[:, a, first : first + P],
+                        out=bank[:, j - j0 : j - j0 + P],
+                        lhsT=words[:, a, 2 * first : 2 * (first + P)].bitcast(FP4X4),
+                        lhsT_scale=scales[:, a, first : first + P],
                         rhs=x_codes[:, cols].bitcast(FP8X4),
                         rhs_scale=x_scales[:, cols],
-                        start=(a == 0 and c0 == j0),
+                        start=(a == 0 and j == j0),
                         stop=False,
                     )
             nc.tensor.matmul_mx(
@@ -239,93 +239,86 @@ def tile_list_hscat_l_silu_kernel(tc, x, w4_words, w4_scales, down, up, b, wgo, 
                 start=False,
                 stop=True,
             )
-
-        def activate(n, src, dst):
-            nc.scalar.activation(dst, src, SILU, bias=bias[:, n : n + 1])
+            nc.scalar.activation(dst, bank[:, 0 : j1 - j0], SILU, bias=bias[:, n : n + 1])
 
         def place(page, j0, j1, src):
-            nc.vector.tensor_tensor(
-                page[:].indirect(lists[:, j0 // LIST_ROWS : j1 // LIST_ROWS]), src, weights[:, j0:j1], MULT
-            )
+            offsets = lists[:, j0 // LIST_ROWS : j1 // LIST_ROWS]
+            nc.vector.tensor_tensor(page[:].indirect(offsets), src, weights[:, j0:j1], MULT)
 
         def store(n, page):
             nc.sync.dma_start(out[n * P : (n + 1) * P, :], page[:])
 
-        weave_down("scalar", 0, 0, P)
+        def late_page(i):
+            page = keep.tile([P, T], F32, name="late_page%d" % i, tag="late%d" % i, align_bytes=64)
+            for c0 in range(0, T, BANK):
+                nc.gpsimd.memset(page[:, c0 : c0 + BANK].bitcast(U32), 0)
+            return page
+
+        weave_down(nc.scalar.copy, 0, 0, P)
         quantise_down(0)
-        weave_x("scalar", 0, 0, 0, W)
-        weave_down("vector", 1, 0, 96)
-        weave_down("scalar", 1, 96, P)
-        quantise_x(0, 0, W)
+        weave_x(nc.scalar.copy, 0, 0, 0, W)
+        weave_down(nc.vector.tensor_copy, 1, 0, DOWN_ON_VECTOR)
+        weave_down(nc.scalar.copy, 1, DOWN_ON_VECTOR, P)
+        quantise_x(x_stage(0, 0, 0, W), 0, 0, 0)
         quantise_down(1)
-        weave_x("scalar", 0, 1, 0, P)
-        quantise_x(0, W, W + P)
-        weave_x("vector", 0, 1, P, W)
-        quantise_x(0, W + P, 2 * W)
-        weave_x("vector", 1, 0, 0, W)
-        quantise_x(1, 0, W)
-        weave_early_up("vector", 0, up_stage[:, 0 : PACK * P])
-        quantise_early_up(0, up_stage[:, 0 : PACK * P])
+        weave_x(nc.scalar.copy, 0, 1, 0, P)
+        quantise_x(x_stage(0, 1, 0, P), 0, 1, 0)
+        weave_x(nc.vector.tensor_copy, 0, 1, P, W)
+        quantise_x(x_stage(0, 1, P, W), 0, 1, P)
+        weave_x(nc.vector.tensor_copy, 1, 0, 0, W)
+        quantise_x(x_stage(1, 0, 0, W), 1, 0, 0)
+        prepare_early_up(0, up_stage[:, 0:K_PASS])
         for r in range(ROUNDS - 2, ROUNDS):
             load_x(r, 0)
             load_x(r, 1)
-        nc.sync.dma_start(w4_rest[:].bitcast(I32), w4_by_part[:, :, 2 * head_cols : 2 * M].bitcast(I32))
+        load_w4(w4_late, EARLY_COLS, M)
         for i in range(2, len(UP_PARTS)):
             load_up(i)
-        load_plane(plane_rest, head_cols, M)
+        load_w4_scales(w4_scales_late, EARLY_COLS, M)
         make_h(0)
-        weave_early_up("vector", 1, up_stage[:, PACK * P :])
-        quantise_early_up(1, up_stage[:, PACK * P :])
-        weave("vector", middle[0], x_raw[1, 1], 0, W)
-        quantise(middle[0], x_codes[:, x_cols(1, W, W)], x_scales[:, x_cols(1, W, W)])
-        weave_early_up("vector", 2, middle[0][:, PACK * P :])
-        quantise_early_up(2, middle[0][:, PACK * P :])
+        prepare_early_up(1, up_stage[:, K_PASS:])
+        weave(nc.vector.tensor_copy, middle[0], x_raw[1, 1], 0, W)
+        quantise_x(middle[0], 1, 1, 0)
+        prepare_early_up(2, middle[0][:, K_PASS:])
+        pages.append(late_page(0))
 
-        def ahead(r, a):
+        def prepare_ahead(r, a):
             if r < ROUNDS:
-                weave_x("scalar", r, a, 0, W)
+                weave_x(nc.scalar.copy, r, a, 0, W)
                 if a == 1:
-                    quantise_x(r, 0, PASSES * W)
+                    quantise_x(stage[r % 2][:], r, 0, 0)
             elif r == ROUNDS:
-                weave("scalar", stage[r % 2][:, a * half :], up_raw[2 + a], 0, W)
+                weave(nc.scalar.copy, x_stage(r, a, 0, W), up_raw[2 + a], 0, W)
                 if a == 1:
-                    cols = slice(UP_PARTS[2][0], UP_PARTS[3][1])
-                    quantise(stage[r % 2][:], up_codes[:, cols], up_scales[:, cols])
+                    quantise_up(stage[r % 2][:], UP_PARTS[2][0])
             elif a == 1:
-                n0, n1 = UP_PARTS[4]
-                weave("scalar", stage[r % 2][:], up_raw[4], 0, n1 - n0)
-                quantise(stage[r % 2][:, 0 : PACK * (n1 - n0)], up_codes[:, n0:n1], up_scales[:, n0:n1])
+                weave(nc.scalar.copy, x_stage(r, 0, 0, P), up_raw[-1], 0, P)
+                quantise_up(x_stage(r, 0, 0, P), UP_PARTS[-1][0])
 
-        second_halves = [x_raw[r, 1] for r in range(1, ROUNDS)] + [up_raw[3]]
+        read_last = [x_raw[r, 1] for r in range(2, ROUNDS)] + [up_raw[3]]
+        parked = [acts[0][:]] + read_last
         for r in range(ROUNDS):
             j0, j1 = r * W, (r + 1) * W
             for n in range(2):
                 bank = h_banks[n] if r == 0 else y_banks[n]
-                held = acts[0][:, 0:W] if r == 0 and n == 0 else second_halves[r][:, n * W : (n + 1) * W]
-                make_y(n, j0, j1, bank[:, 0:W])
-                activate(n, bank[:, 0:W], held)
-                place(pages[n], j0, j1, held)
+                act = parked[r][:, n * W : (n + 1) * W]
+                make_act(n, j0, j1, bank, act)
+                place(pages[n], j0, j1, act)
                 if r == ROUNDS - 1:
                     store(n, pages[n])
-            ahead(r + 2, 0)
+            prepare_ahead(r + 2, 0)
             if r + 1 < ROUNDS:
                 make_h(r + 1)
-            bank = h_banks[j1 // P % 4]
-            make_y(2, j0, j1, bank[:, 0:W])
-            activate(2, bank[:, 0:W], acts[1][:, j0:j1])
+            make_act(2, j0, j1, h_banks[j1 // P % len(h_banks)], acts[1][:, j0:j1])
             place(pages[2], j0, j1, acts[1][:, j0:j1])
-            ahead(r + 2, 1)
+            prepare_ahead(r + 2, 1)
         store(2, pages[2])
 
-        last_page = keep.tile([P, T], F32, name="last_page", tag="last_page", align_bytes=64)
-        for c0 in range(0, T, W):
-            nc.gpsimd.memset(last_page[:, c0 : c0 + W].bitcast(U32), 0)
-        ring = [last_page] + pages
+        ring = [late_page(1)] + pages
         for n in range(EARLY, M // P):
-            act = acts[(n - EARLY) % 2]
+            act = acts[(n - EARLY) % len(acts)]
             page = ring[(n - EARLY) % len(ring)]
-            for q in range(S // BANK):
-                make_y(n, q * BANK, (q + 1) * BANK, y_banks[q][:])
-                activate(n, y_banks[q][:], act[:, q * BANK : (q + 1) * BANK])
+            for q, bank in enumerate(y_banks):
+                make_act(n, q * BANK, (q + 1) * BANK, bank, act[:, q * BANK : (q + 1) * BANK])
             place(page, 0, S, act[:])
             store(n, page)

from contextlib import ExitStack

import concourse.mybir as mybir
from concourse.masks import make_identity

K, M, T, S, R = 1024, 1024, 4096, 2048, 512
FLOPS = 2 * S * (K * R + K * M + R * M)

F32 = mybir.dt.float32
BF16 = mybir.dt.bfloat16
I32 = mybir.dt.int32
U32 = mybir.dt.uint32
U16 = mybir.dt.uint16
U8 = mybir.dt.uint8
FP8X4 = mybir.dt.float8_e4m3fn_x4
FP4X4 = mybir.dt.float4_e2m1fn_x4
SILU = mybir.ActivationFunctionType.Silu
IDENTITY = mybir.ActivationFunctionType.Identity
MULT = mybir.AluOpType.mult

P = 128
PACK = 4
K_PASS = P * PACK
PASSES = K // K_PASS
BANK = 512
QUADRANTS = 4
LIST_ROWS = 16
LINE = 4
W = 256
ROUNDS = S // W
HALF = PACK * W
EARLY = 3
EARLY_COLS = EARLY * P
UP_PARTS = [(0, 256), (256, 384), (384, 640), (640, 896), (896, 1024)]
DOWN_ON_VECTOR = 96


def tile_list_hscat_l_silu_kernel(tc, x, w4_words, w4_scales, down, up, b, wgo, offs, out):
    nc = tc.nc
    with ExitStack() as ctx:
        keep = ctx.enter_context(tc.tile_pool(name="keep", bufs=1))
        psum = ctx.enter_context(tc.psum_pool(name="psum", bufs=1))

        def sbuf(name, shape, dtype):
            return keep.tile(shape, dtype, name=name, align_bytes=64)

        def slots(ap):
            return ap.rearrange("p (t c) -> p t c", t=PACK)

        lists = keep.tile([P, S // LIST_ROWS], U16, name="lists")
        pages = [sbuf("page%d" % i, [P, T], F32) for i in range(2)]
        acts = [sbuf("act%d" % i, [P, S], F32) for i in range(2)]
        weights = sbuf("weights", [P, S], F32)
        down_then_x = sbuf("down_then_x", [P, T], F32)
        x_pairs = [keep.tile([P, T], F32, name="x_pair%d" % i, tag="late%d" % i, align_bytes=64) for i in range(2)]
        down_raw = [down_then_x[:, a * PACK * R : (a + 1) * PACK * R] for a in range(PASSES)]
        x_raw = {}
        for r in range(ROUNDS):
            for a in range(PASSES):
                first = (PASSES * (r % 2) + a) * HALF
                if r < 2 * len(x_pairs):
                    x_raw[r, a] = x_pairs[r // 2][:, first : first + HALF]
                elif r < ROUNDS - 2:
                    x_raw[r, a] = sbuf("x_raw%d_%d" % (r, a), [P, HALF], F32)[:]
                else:
                    x_raw[r, a] = down_then_x[:, first : first + HALF]
        up_raw = [sbuf("up_raw%d" % i, [P, PACK * (n1 - n0)], F32)[:] for i, (n0, n1) in enumerate(UP_PARTS)]
        stage = [sbuf("stage%d" % i, [P, PASSES * HALF], BF16) for i in range(2)]
        down_stage = [sbuf("down_stage%d" % a, [P, PACK * R], BF16) for a in range(PASSES)]
        up_stage = sbuf("up_stage", [P, 2 * K_PASS], BF16)
        h_stage = [sbuf("h_stage%d" % i, [P, HALF], BF16) for i in range(2)]
        x_codes = sbuf("x_codes", [P, PASSES * S], U32)
        x_scales = sbuf("x_scales", [P, PASSES * S], U8)
        down_codes = [sbuf("down_codes%d" % a, [P, R], U32) for a in range(PASSES)]
        down_scales = [sbuf("down_scales%d" % a, [P, R], U8) for a in range(PASSES)]
        h_codes = sbuf("h_codes", [P, S], U32)
        h_scales = sbuf("h_scales", [P, S], U8)
        up_codes = sbuf("up_codes", [P, M], U32)
        up_scales = sbuf("up_scales", [P, M], U8)
        w4_early = sbuf("w4_early", [P, PASSES, 2 * EARLY_COLS], U8)
        w4_late = sbuf("w4_late", [P, PASSES, 2 * (M - EARLY_COLS)], U8)
        w4_scales_early = sbuf("w4_scales_early", [P, PASSES, EARLY_COLS], U8)
        w4_scales_late = sbuf("w4_scales_late", [P, PASSES, M - EARLY_COLS], U8)
        b_rows = sbuf("b_rows", [P, P], F32)
        ident = sbuf("ident", [P, P], F32)
        bias = sbuf("bias", [P, M // P], F32)
        h_banks = [psum.tile([P, BANK], F32, name="h_bank%d" % i) for i in range(4)]
        y_banks = [psum.tile([P, BANK], F32, name="y_bank%d" % i) for i in range(S // BANK)]

        nc.gpsimd.memset(w4_scales_early[:].rearrange("p a n -> p (a n)").bitcast(U32), 0)
        nc.gpsimd.memset(b_rows[:], 0.0)
        nc.vector.memset(w4_scales_late[:].rearrange("p a n -> p (a n)").bitcast(U32), 0)
        for page in pages:
            nc.vector.memset(page[:].bitcast(U32), 0)
        make_identity(nc, ident[:])

        def by_word(rows):
            return rows.rearrange("(p t) c -> p t c", t=PACK)

        def load_down(a):
            nc.sync.dma_start(slots(down_raw[a]), by_word(down[a * K_PASS : (a + 1) * K_PASS, :]))

        def load_x(r, a):
            nc.sync.dma_start(slots(x_raw[r, a]), by_word(x[a * K_PASS : (a + 1) * K_PASS, r * W : (r + 1) * W]))

        def load_up(i):
            n0, n1 = UP_PARTS[i]
            nc.sync.dma_start(slots(up_raw[i]), by_word(up[:, n0:n1]))

        def load_w4(tile, n0, n1):
            words = w4_words.rearrange("a p c -> p a c")[:, :, 2 * n0 : 2 * n1]
            nc.sync.dma_start(tile[:].bitcast(I32), words.bitcast(I32))

        def load_w4_scales(tile, n0, n1):
            for q in range(QUADRANTS):
                nc.sync.dma_start(
                    tile[32 * q : 32 * q + 4, :, :].bitcast(I32),
                    w4_scales[:, 4 * q : 4 * q + 4, n0:n1].rearrange("a r n -> r a n").bitcast(I32),
                )

        def load_weights(j0, j1):
            nc.sync.dma_start(weights[:, j0:j1], wgo[:, j0:j1])

        load_down(0)
        nc.sync.dma_start(b_rows[0 : M // P, :], b.rearrange("(c q) -> c q", q=P))
        load_w4_scales(w4_scales_early, 0, EARLY_COLS)
        nc.sync.dma_start(lists[:], offs)
        load_x(0, 0)
        load_down(1)
        load_x(0, 1)
        load_x(1, 0)
        load_up(0)
        load_w4(w4_early, 0, EARLY_COLS)
        load_x(1, 1)
        load_weights(0, 2 * W)
        load_up(1)
        for r in (2, 3):
            load_x(r, 0)
            load_x(r, 1)
        load_weights(2 * W, S)
        for r in range(4, ROUNDS - 2):
            load_x(r, 0)
            load_x(r, 1)

        nc.tensor.transpose(y_banks[-1][:, 0:P], b_rows[:], ident[:])
        nc.scalar.copy(bias[:], y_banks[-1][:, 0 : M // P])

        def quantise(src, codes, scales):
            nc.vector.quantize_mx(out=codes.bitcast(FP8X4), scales=scales, in_=src)

        def weave(copy, dst, raw, c0, c1):
            copy(
                dst.rearrange("p (c i t) -> p c t i", i=LINE, t=PACK),
                slots(raw)[:, :, c0:c1].rearrange("p t (c i) -> p c t i", i=LINE),
            )

        def weave_down(copy, a, m0, m1):
            copy(
                down_stage[a][:].rearrange("p (u m t) -> p m t u", u=PACK, t=PACK)[:, m0:m1],
                down_raw[a].rearrange("p (t m u) -> p m t u", u=PACK, t=PACK)[:, m0:m1],
            )

        def quantise_down(a):
            quantise(down_stage[a][:], down_codes[a][:], down_scales[a][:])

        def x_cols(a, j0, width):
            first = (j0 // W * PASSES + a) * W + j0 % W
            return slice(first, first + width)

        def x_stage(r, a, c0, c1):
            return stage[r % 2][:, a * HALF + PACK * c0 : a * HALF + PACK * c1]

        def weave_x(copy, r, a, c0, c1):
            weave(copy, x_stage(r, a, c0, c1), x_raw[r, a], c0, c1)

        def quantise_x(src, r, a, c0):
            cols = x_cols(a, r * W + c0, src.shape[1] // PACK)
            quantise(src, x_codes[:, cols], x_scales[:, cols])

        def quantise_up(src, n0):
            cols = slice(n0, n0 + src.shape[1] // PACK)
            quantise(src, up_codes[:, cols], up_scales[:, cols])

        def prepare_early_up(n, dst):
            part = 0 if n * P < UP_PARTS[0][1] else 1
            first = n * P - UP_PARTS[part][0]
            weave(nc.vector.tensor_copy, dst, up_raw[part], first, first + P)
            quantise_up(dst, n * P)

        middle = [tile[:, HALF // 2 : HALF // 2 + HALF] for tile in stage]

        def make_h(r):
            tile = middle[r] if r < len(middle) else h_stage[r % 2][:]
            for j0 in range(r * W, (r + 1) * W, P):
                bank = h_banks[j0 // P % len(h_banks)]
                for a in range(PASSES):
                    cols = x_cols(a, j0, P)
                    for u in range(PACK):
                        nc.tensor.matmul_mx(
                            out=bank[:, u * P : (u + 1) * P],
                            lhsT=down_codes[a][:, u * P : (u + 1) * P].bitcast(FP8X4),
                            lhsT_scale=down_scales[a][:, u * P : (u + 1) * P],
                            rhs=x_codes[:, cols].bitcast(FP8X4),
                            rhs_scale=x_scales[:, cols],
                            start=(a == 0 and u == 0),
                            stop=(a == PASSES - 1 and u == PACK - 1),
                        )
                copy = nc.vector.tensor_copy if j0 == P else nc.scalar.copy
                copy(
                    tile[:, PACK * (j0 % W) : PACK * (j0 % W + P)].rearrange("p (c u) -> p c u", u=PACK),
                    bank[:].rearrange("p (u c) -> p c u", u=PACK),
                )
            quantise(tile, h_codes[:, r * W : (r + 1) * W], h_scales[:, r * W : (r + 1) * W])

        def make_act(n, j0, j1, bank, dst):
            n0 = n * P
            if n < EARLY:
                words, scales, first = w4_early, w4_scales_early, n0
            else:
                words, scales, first = w4_late, w4_scales_late, n0 - EARLY_COLS
            for a in range(PASSES):
                for j in range(j0, j1, P):
                    cols = x_cols(a, j, P)
                    nc.tensor.matmul_mx(
                        out=bank[:, j - j0 : j - j0 + P],
                        lhsT=words[:, a, 2 * first : 2 * (first + P)].bitcast(FP4X4),
                        lhsT_scale=scales[:, a, first : first + P],
                        rhs=x_codes[:, cols].bitcast(FP8X4),
                        rhs_scale=x_scales[:, cols],
                        start=(a == 0 and j == j0),
                        stop=False,
                    )
            nc.tensor.matmul_mx(
                out=bank[:, 0 : j1 - j0],
                lhsT=up_codes[:, n0 : n0 + P].bitcast(FP8X4),
                lhsT_scale=up_scales[:, n0 : n0 + P],
                rhs=h_codes[:, j0:j1].bitcast(FP8X4),
                rhs_scale=h_scales[:, j0:j1],
                start=False,
                stop=True,
            )
            nc.scalar.activation(dst, bank[:, 0 : j1 - j0], SILU, bias=bias[:, n : n + 1])

        def place(page, j0, j1, src):
            offsets = lists[:, j0 // LIST_ROWS : j1 // LIST_ROWS]
            nc.vector.tensor_tensor(page[:].indirect(offsets), src, weights[:, j0:j1], MULT)

        def store(n, page):
            nc.sync.dma_start(out[n * P : (n + 1) * P, :], page[:])

        def late_page(i):
            page = keep.tile([P, T], F32, name="late_page%d" % i, tag="late%d" % i, align_bytes=64)
            for c0 in range(0, T, BANK):
                nc.gpsimd.memset(page[:, c0 : c0 + BANK].bitcast(U32), 0)
            return page

        weave_down(nc.scalar.copy, 0, 0, P)
        quantise_down(0)
        weave_x(nc.scalar.copy, 0, 0, 0, W)
        weave_down(nc.vector.tensor_copy, 1, 0, DOWN_ON_VECTOR)
        weave_down(nc.scalar.copy, 1, DOWN_ON_VECTOR, P)
        quantise_x(x_stage(0, 0, 0, W), 0, 0, 0)
        quantise_down(1)
        weave_x(nc.scalar.copy, 0, 1, 0, P)
        quantise_x(x_stage(0, 1, 0, P), 0, 1, 0)
        weave_x(nc.vector.tensor_copy, 0, 1, P, W)
        quantise_x(x_stage(0, 1, P, W), 0, 1, P)
        weave_x(nc.vector.tensor_copy, 1, 0, 0, W)
        quantise_x(x_stage(1, 0, 0, W), 1, 0, 0)
        prepare_early_up(0, up_stage[:, 0:K_PASS])
        for r in range(ROUNDS - 2, ROUNDS):
            load_x(r, 0)
            load_x(r, 1)
        load_w4(w4_late, EARLY_COLS, M)
        for i in range(2, len(UP_PARTS)):
            load_up(i)
        load_w4_scales(w4_scales_late, EARLY_COLS, M)
        make_h(0)
        prepare_early_up(1, up_stage[:, K_PASS:])
        weave(nc.vector.tensor_copy, middle[0], x_raw[1, 1], 0, W)
        quantise_x(middle[0], 1, 1, 0)
        prepare_early_up(2, middle[0][:, K_PASS:])
        pages.append(late_page(0))

        def prepare_ahead(r, a):
            if r < ROUNDS:
                weave_x(nc.scalar.copy, r, a, 0, W)
                if a == 1:
                    quantise_x(stage[r % 2][:], r, 0, 0)
            elif r == ROUNDS:
                weave(nc.scalar.copy, x_stage(r, a, 0, W), up_raw[2 + a], 0, W)
                if a == 1:
                    quantise_up(stage[r % 2][:], UP_PARTS[2][0])
            elif a == 1:
                weave(nc.scalar.copy, x_stage(r, 0, 0, P), up_raw[-1], 0, P)
                quantise_up(x_stage(r, 0, 0, P), UP_PARTS[-1][0])

        read_last = [x_raw[r, 1] for r in range(2, ROUNDS)] + [up_raw[3]]
        parked = [acts[0][:]] + read_last
        for r in range(ROUNDS):
            j0, j1 = r * W, (r + 1) * W
            for n in range(2):
                bank = h_banks[n] if r == 0 else y_banks[n]
                act = parked[r][:, n * W : (n + 1) * W]
                make_act(n, j0, j1, bank, act)
                place(pages[n], j0, j1, act)
                if r == ROUNDS - 1:
                    store(n, pages[n])
            prepare_ahead(r + 2, 0)
            if r + 1 < ROUNDS:
                make_h(r + 1)
            make_act(2, j0, j1, h_banks[j1 // P % len(h_banks)], acts[1][:, j0:j1])
            place(pages[2], j0, j1, acts[1][:, j0:j1])
            prepare_ahead(r + 2, 1)
        store(2, pages[2])

        ring = [late_page(1)] + pages
        for n in range(EARLY, M // P):
            act = acts[(n - EARLY) % len(acts)]
            page = ring[(n - EARLY) % len(ring)]
            for q, bank in enumerate(y_banks):
                make_act(n, q * BANK, (q + 1) * BANK, bank, act[:, q * BANK : (q + 1) * BANK])
            place(page, 0, S, act[:])
            store(n, page)
